import numpy as np
import ml_dtypes


def mxq(x, axis, fmt="e4m3"):
    dtype, down = {"e4m3": (ml_dtypes.float8_e4m3fn, 7), "e5m2": (ml_dtypes.float8_e5m2, 14)}[fmt]
    v = np.moveaxis(np.asarray(x, np.float32).astype(ml_dtypes.bfloat16).astype(np.float64), axis, -1)
    blocks = v.reshape(v.shape[:-1] + (-1, 32))
    amax = np.abs(blocks).max(-1, keepdims=True)
    byte = np.maximum(np.where(amax > 0, np.frexp(amax)[1] - 1 + 127, 0) - down, 1)
    scale = np.exp2(byte - 127.0)
    codes = (blocks / scale).astype(np.float32).astype(dtype).astype(np.float64)
    return np.moveaxis((codes * scale).reshape(v.shape), -1, axis)


WIDE = False


def mx_kscale(k):
    if not WIDE:
        return np.ones(k)
    levels = np.array([10, -10, 5, -5, 0])
    if k % 512:
        return np.exp2(np.random.permutation(np.resize(levels, k // 32))).repeat(32)
    a = np.empty((k // 512, 16))
    for p in range(k // 512):
        a[p, :8] = np.random.permutation(np.resize(levels, 8))
        for g in range(8):
            far = levels[np.abs(levels - a[p, g]) >= 10]
            a[p, g + 8] = far[np.random.randint(len(far))]
    return np.exp2(a.ravel()).repeat(32)


def f64(x):
    return np.asarray(x).astype(np.float64)


def striped(idx):
    return np.tile(idx.reshape(-1, 16).T, (8, 1)).astype(np.uint16)


def unstriped(offs):
    return offs[:16].T.reshape(-1).astype(np.int64)


def striped8(idx):
    return np.concatenate([x.reshape(-1, 16).T for x in idx]).astype(np.uint16)


def runs(offs, k):
    lists = np.stack([offs[16 * r : 16 * r + 16].T.reshape(-1) for r in range(8)]).astype(np.int64)
    return lists[np.arange(k) % 512 // 64]


def pack_weight(w):
    k, n = w.shape
    w = f64(np.asarray(w, np.float32).astype(ml_dtypes.bfloat16)).reshape(k // 32, 32, n)
    amax = np.abs(w).max(1)
    byte = np.clip(np.where(amax > 0, np.frexp(amax)[1] - 1 + 127 - 7, 1), 1, 254)
    scaled = (w * np.exp2(127.0 - byte)[:, None, :]).reshape(k, n).astype(np.float32)
    words = np.ascontiguousarray(scaled.reshape(k // 512, 128, 4, n).transpose(0, 1, 3, 2)).astype(ml_dtypes.float8_e4m3fn).view(np.uint8)
    return words, np.ascontiguousarray(byte.astype(np.uint8).reshape(k // 512, 16, n))


def unpack_weight(words, scales):
    g, p, n, _ = words.shape
    vals = np.ascontiguousarray(words).view(ml_dtypes.float8_e4m3fn).astype(np.float64) * np.repeat(np.exp2(scales.astype(np.float64) - 127.0), 8, axis=1)[..., None]
    return vals.transpose(0, 1, 3, 2).reshape(g * 512, n)


K, T, S, H, G = 512, 1024, 512, 512, 2048


def setup_inputs():
    n = np.random.standard_normal
    s = mx_kscale(K)[:, None]
    packed_xT = pack_weight(n((K, T)) * s)
    packed_dT = pack_weight(n((K, G)) / s)
    return {
        "x_words": packed_xT[0],
        "x_scales": packed_xT[1],
        "w1": (n((K, H)) / np.sqrt(K) / s).astype(np.float32),
        "w2": (n((K, H)) / np.sqrt(K) / s).astype(np.float32),
        "gs": (np.random.uniform(0.5, 1.5, (K, 1)) * s).astype(np.float32),
        "d_words": packed_dT[0],
        "d_scales": packed_dT[1],
        "offs": striped(np.random.permutation(T)[:S]),
        "two": striped(np.random.permutation(T)[:S]),
        "n1": striped8(np.stack([np.random.permutation(S) for _ in range(8)])),
        "n2": striped8(np.stack([np.random.permutation(S) for _ in range(8)])),
        "n3": striped8(np.stack([np.random.permutation(S) for _ in range(8)])),
        "k1": striped8(np.random.randint(0, G, (8, H))),
        "n4": striped8(np.stack([np.random.permutation(S) for _ in range(8)])),
        "n5": striped8(np.stack([np.random.permutation(S) for _ in range(8)])),
    }


def reference(x_words, x_scales, w1, w2, gs, d_words, d_scales, offs, two, n1, n2, n3, k1, n4, n5):
    d_k1 = unpack_weight(d_words, d_scales)[np.arange(K)[:, None], runs(k1, K)]
    x_two = unpack_weight(x_words, x_scales)[:, unstriped(two)]
    d = mxq(f64(w2), 0, "e4m3").T @ x_two
    xq = unpack_weight(x_words, x_scales)[:, unstriped(offs)]
    y = mxq(f64(w1), 0, "e4m3").T @ xq
    z = f64(gs) * (d * (y[np.arange(H)[:, None], runs(n1, H)] - y) + 0.5 * ((d[np.arange(H)[:, None], runs(n3, H)]) * (y[np.arange(H)[:, None], runs(n2, H)] - y)))
    h = 0.0625 * ((d_k1.T @ mxq(z, 0, "e4m3")))
    pa = h[np.arange(H)[:, None], runs(n4, H)]
    pb = h[np.arange(H)[:, None], runs(n5, H)]
    mu = 0.3125 * (h + pa + pb)
    return (h - mu) / (np.sqrt((pa - mu) ** 2 + (pb - mu) ** 2 + 0.25))

@@ -1,0 +1,316 @@
+from contextlib import ExitStack
+
+import concourse.mybir as mybir
+from concourse.masks import make_identity
+
+F32 = mybir.dt.float32
+BF16 = mybir.dt.bfloat16
+I32 = mybir.dt.int32
+U32 = mybir.dt.uint32
+U16 = mybir.dt.uint16
+U8 = mybir.dt.uint8
+FP8X4 = mybir.dt.float8_e4m3fn_x4
+ACT = mybir.ActivationFunctionType
+ALU = mybir.AluOpType
+
+P = 128
+PACK = 4
+K, T, S, H, G = 512, 1024, 512, 512, 2048
+HALF = S // 2
+FLOPS = 3 * 2 * K * H * S
+
+Z_CHUNKS = [256,128,128]
+
+
+def tile_picked_twqflowbstd_none_p_kernel(
+    tc, x_words, x_scales, w1, w2, gs, d_words, d_scales, offs, two, n1, n2, n3, k1, n4, n5, out
+):
+    nc = tc.nc
+    with ExitStack() as ctx:
+        keep = ctx.enter_context(tc.tile_pool(name="keep", bufs=1))
+        ring = ctx.enter_context(tc.tile_pool(name="ring", bufs=4))
+        psum = ctx.enter_context(tc.psum_pool(name="psum", bufs=1))
+
+        def load_list(src, name):
+            tile = keep.tile([P, S // 16], U16, name=name)
+            nc.sync.dma_start(tile[:], src)
+            return tile
+
+        def entries(lst, c0, n):
+            return lst[:, c0 // 16 : (c0 + n) // 16]
+
+        def gather(engine, dst, window, lst, c0, n):
+            src = window[:].indirect(entries(lst, c0, n))
+            if engine == "scalar":
+                nc.scalar.activation(dst, src, ACT.Copy)
+            else:
+                nc.vector.tensor_copy(dst, src)
+
+        def words_view(dram):
+            return dram[0].rearrange("p c r -> p (c r)").bitcast(I32)
+
+        def load_weight(w, name, u):
+            rows = w.rearrange("(p j) c -> p j c", j=PACK)
+            raw = keep.tile([P, PACK, H // 2], F32, name="%s_raw%d" % (name, u), align_bytes=64)
+            nc.sync.dma_start(raw[:], rows[:, :, u * (H // 2) : (u + 1) * (H // 2)])
+            return raw
+
+        def round_weight(engines, halves, name):
+            grouped = keep.tile([P, PACK * H], BF16, name=name + "_bf", tag="w_bf", align_bytes=64)
+            view = grouped[:].rearrange("p (t m j) -> p m j t", t=PACK, j=PACK)
+            for u in range(2):
+                dst = view[:, u * (P // 2) : (u + 1) * (P // 2), :, :]
+                src = halves[u][:].rearrange("p j (m t) -> p m j t", t=PACK)
+                if engines[u] == "scalar":
+                    nc.scalar.copy(dst, src)
+                elif engines[u] == "vector":
+                    nc.vector.tensor_copy(dst, src)
+                else:
+                    nc.gpsimd.tensor_scalar(dst, src, 1.0, 0.0, ALU.mult, ALU.add)
+            return grouped
+
+        def quantize(grouped, cuts, name):
+            codes = keep.tile([P, cuts[-1]], U32, name=name + "_codes", align_bytes=64)
+            scales = keep.tile([P, cuts[-1]], U8, name=name + "_scales", align_bytes=64)
+            for a, b in zip(cuts, cuts[1:]):
+                nc.vector.quantize_mx(out=codes[:, a:b].bitcast(FP8X4), scales=scales[:, a:b], in_=grouped[:, PACK * a : PACK * b])
+            return codes, scales
+
+        def pick(words, scales, lst, name, tag=None):
+            pw = keep.tile([P, S], U32, name=name + "_words", align_bytes=64)
+            ps = keep.tile([P, S], U8, name=name + "_bytes", tag=tag or name + "_bytes", align_bytes=64)
+            nc.vector.tensor_copy(pw[:], words[:].bitcast(U32).indirect(lst[:]))
+            nc.vector.tensor_copy(ps[:], scales[:].indirect(lst[:]))
+            return pw, ps
+
+        def product(dst, lhs, t, rhs, c0, n):
+            cols = slice(t * P, (t + 1) * P)
+            nc.tensor.matmul_mx(
+                out=dst,
+                lhsT=lhs[0][:, cols].bitcast(FP8X4),
+                lhsT_scale=lhs[1][:, cols],
+                rhs=rhs[0][:, c0 : c0 + n].bitcast(FP8X4),
+                rhs_scale=rhs[1][:, c0 : c0 + n],
+                start=True,
+                stop=True,
+            )
+
+        l_offs = load_list(offs, "l_offs")
+        xw = keep.tile([P, T], I32, name="xw")
+        nc.sync.dma_start(xw[:], words_view(x_words))
+        xs = keep.tile([P, T], U8, name="xs")
+        x_rows = x_scales[0].bitcast(I32).rearrange("(q a) c -> a q c", a=4)
+        for a in range(4):
+            nc.scalar.dma_start(xs[a:P:4, :].bitcast(I32), x_rows[a].unsqueeze(1).to_broadcast([4, 8, T // 4]))
+        w1_raw = [load_weight(w1, "w1", u) for u in range(2)]
+        l_two = load_list(two, "l_two")
+        w2_raw = [load_weight(w2, "w2", 0)]
+        l_n1 = load_list(n1, "l_n1")
+        l_n2 = load_list(n2, "l_n2")
+        w2_raw.append(load_weight(w2, "w2", 1))
+        gain = keep.tile([P, PACK], F32, name="gain")
+        nc.sync.dma_start(gain[:], gs.rearrange("(p t) o -> p (t o)", t=PACK))
+        l_n3 = load_list(n3, "l_n3")
+        dw = keep.tile([P, G], I32, name="dw")
+        nc.sync.dma_start(dw[:], words_view(d_words))
+        ds = keep.tile([P, G], U8, name="ds")
+        nc.gpsimd.memset(ds[:].bitcast(I32), 0)
+        for e in range(2):
+            nc.sync.dma_start(ds[e:P:16, :].bitcast(I32), d_scales[0, e:16:2, :].bitcast(I32))
+        l_k1 = load_list(k1, "l_k1")
+        l_n4 = load_list(n4, "l_n4")
+        l_n5 = load_list(n5, "l_n5")
+
+        ident = keep.tile([P, P], F32, name="ident")
+        make_identity(nc, ident[:])
+        dict_scales = keep.tile([P, H], U8, name="dict_scales", align_bytes=64)
+        nc.gpsimd.memset(dict_scales[:].bitcast(I32), 0)
+
+        def bank(i, name):
+            return psum.tile([P, S], F32, name=name, tag="bank%d" % i)
+
+        def leave(engine, dst, src, scale):
+            if engine == "scalar":
+                nc.scalar.activation(dst, src, ACT.Copy, scale=scale)
+            else:
+                nc.vector.tensor_scalar(dst, src, scale, None, ALU.mult)
+
+        x_offs = pick(xw, xs, l_offs, "x_offs")
+        w1_q = quantize(round_weight(["scalar","scalar"], w1_raw, "w1"), [0, P, H], "w1")
+        y_bank = [bank(t, "y_bank%d" % t) for t in range(PACK)]
+        y_win = [keep.tile([P, S], F32, name="y_win%d" % t) for t in range(PACK)]
+        for t in range(PACK):
+            product(y_bank[t][:], w1_q, t, x_offs, 0, S)
+            leave("vector" if t else "scalar", y_win[t][:], y_bank[t][:], 1.0)
+
+        x_two = pick(xw, xs, l_two, "x_two", "w1_raw1")
+        w2_q = quantize(round_weight(["gpsimd","gpsimd"], w2_raw, "w2"), [0, H], "w2")
+        half_gain = keep.tile([P, PACK], F32, name="half_gain")
+        nc.vector.tensor_scalar(half_gain[:], gain[:], 0.5, None, ALU.mult)
+        d_bank = [bank(PACK + t, "d_bank%d" % t) for t in range(PACK)]
+        d_win = [keep.tile([P, S], F32, name="d_win%d" % t) for t in range(PACK)]
+        for t in range(PACK):
+            product(d_bank[t][:], w2_q, t, x_two, 0, S)
+
+        def pick_dictionary():
+            dk_words, dk_bytes = pick(dw, ds, l_k1, "dk")
+            words = keep.tile([P, H], U32, name="dict_words", align_bytes=64)
+            nc.vector.tensor_copy(words[:].rearrange("p (t m) -> p m t", t=PACK), dk_words[:].rearrange("p (m t) -> p m t", t=PACK))
+            dealt = keep.tile([P, H], U8, name="dealt_bytes", align_bytes=64)
+            nc.vector.tensor_copy(dealt[:].rearrange("p (t m) -> p t m", t=PACK), dk_bytes[:].rearrange("p (m t) -> p t m", t=PACK))
+            for a in range(4):
+                nc.sync.dma_start(
+                    dict_scales[a:P:32, :].bitcast(I32), dealt[16 * (a // 2) + a % 2 : P : 32, :].bitcast(I32)
+                )
+            return words, dict_scales
+
+        dictionary = None
+        z_q = []
+        sums = []
+        c0 = 0
+        for ci, n in enumerate(Z_CHUNKS):
+            last = ci == len(Z_CHUNKS) - 1
+            near = keep.tile([P, PACK, n], F32, name="near%d" % ci)
+            far = keep.tile([P, PACK, n], F32, name="far%d" % ci)
+            sums.append((near, far))
+            diffs, d3s = [], []
+
+            def fetch_y(t):
+                y12 = ring.tile([P, 2, n], F32, name="y12", tag="y12", bufs=4)
+                gather("scalar", y12[:, 0, :], y_win[t], l_n1, c0, n)
+                gather("scalar", y12[:, 1, :], y_win[t], l_n2, c0, n)
+                if False:
+                    diff = sums[0][0][:, t, :].rearrange("p (s n) -> p s n", s=2)
+                else:
+                    diff_tile = keep.tile([P, 2, n], F32, name="diff%d%d" % (ci, t))
+                    diff = diff_tile[:]
+                if False:
+                    nc.gpsimd.tensor_tensor(diff, y12[:], y_win[t][:, c0 : c0 + n].unsqueeze(1).to_broadcast([P, 2, n]), ALU.subtract)
+                else:
+                    nc.vector.tensor_tensor(diff, y12[:], y_bank[t][:, c0 : c0 + n].unsqueeze(1).to_broadcast([P, 2, n]), ALU.subtract)
+                diffs.append(diff)
+
+            def fetch_d(t):
+                d3 = ring.tile([P, n], F32, name="d3", tag="d3", bufs=4)
+                gather("scalar", d3[:], d_win[t], l_n3, c0, n)
+                d3s.append(d3)
+
+            def weigh(t):
+                nc.vector.scalar_tensor_tensor(
+                    near[:, t, :], d_bank[t][:, c0 : c0 + n], gain[:, t : t + 1], diffs[t][:, 0, :], ALU.mult, ALU.mult
+                )
+                far_engine = nc.vector
+                far_engine.tensor_tensor(far[:, t, :], d3s[t][:], diffs[t][:, 1, :], ALU.mult)
+
+            if ci == 0:
+                for t in range(PACK):
+                    fetch_y(t)
+                dictionary = pick_dictionary()
+                for t in range(PACK):
+                    leave("scalar", d_win[t][:], d_bank[t][:], half_gain[:, t : t + 1])
+                for t in range(PACK):
+                    fetch_d(t)
+                    weigh(t)
+            else:
+                for t in range(PACK):
+                    fetch_d(t)
+                    fetch_y(t)
+                    weigh(t)
+            z_bf = keep.tile([P, n * PACK], BF16, name="z_bf%d" % ci, align_bytes=64)
+            z_engine = nc.vector
+            z_engine.tensor_tensor(
+                z_bf[:].rearrange("p (c i t) -> p c t i", i=4, t=PACK),
+                near[:].rearrange("p t (c i) -> p c t i", i=4),
+                far[:].rearrange("p t (c i) -> p c t i", i=4),
+                ALU.add,
+            )
+            z_q.append((quantize(z_bf, [0, n], "z%d" % ci), c0, n))
+            c0 = c0 + n
+
+        h_bank = [bank(t, "h_bank%d" % t) for t in range(PACK)]
+        h_win = [keep.tile([P, S], F32, name="h_win%d" % t) for t in range(PACK)]
+        early = S - Z_CHUNKS[-1]
+        for t in range(PACK):
+            for zq, c0, n in z_q[:-1]:
+                product(h_bank[t][:, c0 : c0 + n], dictionary, t, zq, 0, n)
+            leave("scalar", h_win[t][:, :early], h_bank[t][:, :early], 0.0625)
+        for t in range(PACK):
+            product(h_bank[t][:, early:], dictionary, t, z_q[-1][0], 0, S - early)
+            leave("vector" if t % 2 else "scalar", h_win[t][:, early:], h_bank[t][:, early:], 0.0625)
+
+        out_rows = out.rearrange("(p t) n -> p t n", t=PACK)
+        pieces = [(t, c0, HALF) for t in range(PACK) for c0 in (0, HALF)]
+        count = len(pieces)
+        used = {"both": {}, "apart": {}}
+
+        def fetch(i):
+            t, c0, n = pieces[i]
+            pa = ring.tile([P, n], F32, name="pa")
+            pb = ring.tile([P, n], F32, name="pb")
+            gather("scalar", pa[:], h_win[t], l_n4, c0, n)
+            gather("vector", pb[:], h_win[t], l_n5, c0, n)
+            return pa, pb
+
+        def combine(i, pa, pb):
+            t, c0, n = pieces[i]
+            both = keep.tile([P, n], F32, name="both%d" % i)
+            apart = keep.tile([P, n], F32, name="apart%d" % i)
+            used["both"][i], used["apart"][i] = both, apart
+            both_engine = nc.gpsimd
+            apart_engine = nc.gpsimd
+            both_engine.tensor_tensor(both[:], pa[:], pb[:], ALU.add)
+            apart_engine.tensor_tensor(apart[:], pa[:], pb[:], ALU.subtract)
+            return both, apart
+
+        def square(i, both, apart):
+            t, c0, n = pieces[i]
+            h_here = h_bank[t][:, c0 : c0 + n]
+            top = ring.tile([P, n], F32, name="top", bufs=6)
+            mean = ring.tile([P, n], F32, name="mean")
+            nc.vector.scalar_tensor_tensor(mean[:], h_here, -5.0 / 48.0, both[:], ALU.mult, ALU.add)
+            nc.vector.scalar_tensor_tensor(top[:], h_here, -2.2 / 16.0, both[:], ALU.mult, ALU.add)
+            sq = ring.tile([P, 2, n], F32, name="sq")
+            nc.scalar.activation(sq[:, 0, :], apart[:], ACT.Square, scale=0.5**0.5)
+            nc.scalar.activation(sq[:, 1, :], mean[:], ACT.Square, scale=0.375 * 0.5**0.5)
+            if False:
+                total = ring.tile([P, n], F32, name="sum")
+                nc.vector.tensor_tensor(total[:], sq[:, 0, :], sq[:, 1, :], ALU.add)
+                return top, total[:]
+            total = psum.tile([P, n], F32, name="total", tag="bank%d" % (4 + i % 2))
+            for b in range(n // P):
+                for s in range(2):
+                    nc.tensor.matmul(
+                        total[:, b * P : (b + 1) * P], sq[:, s, b * P : (b + 1) * P], ident[:], start=(s == 0), stop=(s == 1), is_transpose=True
+                    )
+            return top, total[:]
+
+        def spent(kind, j, n, name):
+            if j < count and pieces[j][2] == n:
+                return used[kind][j]
+            return ring.tile([P, n], F32, name=name)
+
+        def invert(i, top, total):
+            t, c0, n = pieces[i]
+            root = spent("apart", i + 1, n, "root")
+            nc.scalar.activation(root[:], total, ACT.Abs_reciprocal_sqrt, bias=0.25)
+            if False:
+                return top, root[:]
+            back = psum.tile([P, n], F32, name="back", tag="bank%d" % (6 + i % 2))
+            for b in range(n // P):
+                nc.tensor.transpose(back[:, b * P : (b + 1) * P], root[:, b * P : (b + 1) * P], ident[:])
+            return top, back[:]
+
+        def finish(i, top, back):
+            t, c0, n = pieces[i]
+            res = spent("both", i + 3, n, "res")
+            nc.vector.scalar_tensor_tensor(res[:], top[:], -0.3125, back, ALU.mult, ALU.mult)
+            nc.sync.dma_start(out_rows[:, t, c0 : c0 + n], res[:])
+            return ()
+
+        stages = [(square, 2), (invert, 3), (finish, 5), (combine, 1), (fetch, 0)]
+        state = [()] * count
+        for step in range(count + 5):
+            for stage, lag in stages:
+                i = step - lag
+                if 0 <= i < count:
+                    state[i] = stage(i, *state[i])

@@ -56,7 +56,7 @@ def tile_picked_twqflowbstd_none_p_kernel(
             return raw
 
         def round_weight(engines, halves, name):
-            grouped = keep.tile([P, PACK * H], BF16, name=name + "_bf", tag="w_bf", align_bytes=64)
+            grouped = keep.tile([P, PACK * H], BF16, name=name + "_bf", align_bytes=64)
             view = grouped[:].rearrange("p (t m j) -> p m j t", t=PACK, j=PACK)
             for u in range(2):
                 dst = view[:, u * (P // 2) : (u + 1) * (P // 2), :, :]
@@ -96,14 +96,16 @@ def tile_picked_twqflowbstd_none_p_kernel(
             )
 
         l_offs = load_list(offs, "l_offs")
-        xw = keep.tile([P, T], I32, name="xw")
-        nc.sync.dma_start(xw[:], words_view(x_words))
+        l_two = load_list(two, "l_two")
         xs = keep.tile([P, T], U8, name="xs")
         x_rows = x_scales[0].bitcast(I32).rearrange("(q a) c -> a q c", a=4)
         for a in range(4):
-            nc.scalar.dma_start(xs[a:P:4, :].bitcast(I32), x_rows[a].unsqueeze(1).to_broadcast([4, 8, T // 4]))
-        w1_raw = [load_weight(w1, "w1", u) for u in range(2)]
-        l_two = load_list(two, "l_two")
+            queue = nc.sync if a == 0 else nc.scalar
+            queue.dma_start(xs[a:P:4, :].bitcast(I32), x_rows[a].unsqueeze(1).to_broadcast([4, 8, T // 4]))
+        w1_raw = [load_weight(w1, "w1", 0)]
+        xw = keep.tile([P, T], I32, name="xw")
+        nc.sync.dma_start(xw[:], words_view(x_words))
+        w1_raw.append(load_weight(w1, "w1", 1))
         w2_raw = [load_weight(w2, "w2", 0)]
         l_n1 = load_list(n1, "l_n1")
         l_n2 = load_list(n2, "l_n2")
@@ -143,8 +145,8 @@ def tile_picked_twqflowbstd_none_p_kernel(
             product(y_bank[t][:], w1_q, t, x_offs, 0, S)
             leave("vector" if t else "scalar", y_win[t][:], y_bank[t][:], 1.0)
 
-        x_two = pick(xw, xs, l_two, "x_two", "w1_raw1")
-        w2_q = quantize(round_weight(["gpsimd","gpsimd"], w2_raw, "w2"), [0, H], "w2")
+        x_two = pick(xw, xs, l_two, "x_two")
+        w2_q = quantize(round_weight(["scalar","vector"], w2_raw, "w2"), [0, H], "w2")
         half_gain = keep.tile([P, PACK], F32, name="half_gain")
         nc.vector.tensor_scalar(half_gain[:], gain[:], 0.5, None, ALU.mult)
         d_bank = [bank(PACK + t, "d_bank%d" % t) for t in range(PACK)]
@@ -203,9 +205,9 @@ def tile_picked_twqflowbstd_none_p_kernel(
                 far_engine.tensor_tensor(far[:, t, :], d3s[t][:], diffs[t][:, 1, :], ALU.mult)
 
             if ci == 0:
+                dictionary = pick_dictionary()
                 for t in range(PACK):
                     fetch_y(t)
-                dictionary = pick_dictionary()
                 for t in range(PACK):
                     leave("scalar", d_win[t][:], d_bank[t][:], half_gain[:, t : t + 1])
                 for t in range(PACK):
@@ -248,7 +250,7 @@ def tile_picked_twqflowbstd_none_p_kernel(
             pa = ring.tile([P, n], F32, name="pa")
             pb = ring.tile([P, n], F32, name="pb")
             gather("scalar", pa[:], h_win[t], l_n4, c0, n)
-            gather("vector", pb[:], h_win[t], l_n5, c0, n)
+            gather("scalar" if i in (1, 2) else "vector", pb[:], h_win[t], l_n5, c0, n)
             return pa, pb
 
         def combine(i, pa, pb):
@@ -256,8 +258,8 @@ def tile_picked_twqflowbstd_none_p_kernel(
             both = keep.tile([P, n], F32, name="both%d" % i)
             apart = keep.tile([P, n], F32, name="apart%d" % i)
             used["both"][i], used["apart"][i] = both, apart
-            both_engine = nc.gpsimd
-            apart_engine = nc.gpsimd
+            both_engine = nc.vector if i in (0, count - 1) else nc.gpsimd
+            apart_engine = nc.vector if i in (0, count - 1) else nc.gpsimd
             both_engine.tensor_tensor(both[:], pa[:], pb[:], ALU.add)
             apart_engine.tensor_tensor(apart[:], pa[:], pb[:], ALU.subtract)
             return both, apart
@@ -272,7 +274,7 @@ def tile_picked_twqflowbstd_none_p_kernel(
             sq = ring.tile([P, 2, n], F32, name="sq")
             nc.scalar.activation(sq[:, 0, :], apart[:], ACT.Square, scale=0.5**0.5)
             nc.scalar.activation(sq[:, 1, :], mean[:], ACT.Square, scale=0.375 * 0.5**0.5)
-            if False:
+            if i >= count - 1:
                 total = ring.tile([P, n], F32, name="sum")
                 nc.vector.tensor_tensor(total[:], sq[:, 0, :], sq[:, 1, :], ALU.add)
                 return top, total[:]
@@ -293,7 +295,7 @@ def tile_picked_twqflowbstd_none_p_kernel(
             t, c0, n = pieces[i]
             root = spent("apart", i + 1, n, "root")
             nc.scalar.activation(root[:], total, ACT.Abs_reciprocal_sqrt, bias=0.25)
-            if False:
+            if i >= count - 1:
                 return top, root[:]
             back = psum.tile([P, n], F32, name="back", tag="bank%d" % (6 + i % 2))
             for b in range(n // P):

@@ -17,9 +17,16 @@ P = 128
 PACK = 4
 K, T, S, H, G = 512, 1024, 512, 512, 2048
 HALF = S // 2
+QUARTER = S // 4
+H_SCALE = 0.0625
+WIN_SCALE = 1.0 / (0.625 * H_SCALE)
 FLOPS = 3 * 2 * K * H * S
 
-Z_CHUNKS = [256,128,128]
+WHOLE_TILE = 1
+W1_CUT = 320
+W2_CUT = H // 2
+GPSIMD_DIFFS = 2
+SCALAR_Y, SCALAR_D = 2, 1
 
 
 def tile_picked_twqflowbstd_none_p_kernel(
@@ -28,7 +35,7 @@ def tile_picked_twqflowbstd_none_p_kernel(
     nc = tc.nc
     with ExitStack() as ctx:
         keep = ctx.enter_context(tc.tile_pool(name="keep", bufs=1))
-        ring = ctx.enter_context(tc.tile_pool(name="ring", bufs=4))
+        ring = ctx.enter_context(tc.tile_pool(name="ring", bufs=3))
         psum = ctx.enter_context(tc.psum_pool(name="psum", bufs=1))
 
         def load_list(src, name):
@@ -36,37 +43,21 @@ def tile_picked_twqflowbstd_none_p_kernel(
             nc.sync.dma_start(tile[:], src)
             return tile
 
-        def entries(lst, c0, n):
-            return lst[:, c0 // 16 : (c0 + n) // 16]
+        def load_words(src, columns, name):
+            tile = keep.tile([P, columns], I32, name=name)
+            nc.sync.dma_start(tile[:], src[0].rearrange("p c r -> p (c r)").bitcast(I32))
+            return tile
 
-        def gather(engine, dst, window, lst, c0, n):
-            src = window[:].indirect(entries(lst, c0, n))
-            if engine == "scalar":
-                nc.scalar.activation(dst, src, ACT.Copy)
-            else:
-                nc.vector.tensor_copy(dst, src)
+        def load_weight(w, name, c0, c1):
+            raw = keep.tile([P, PACK, c1 - c0], F32, name=name, align_bytes=64)
+            nc.sync.dma_start(raw[:], w.rearrange("(p j) c -> p j c", j=PACK)[:, :, c0:c1])
+            return raw, c0, c1
 
-        def words_view(dram):
-            return dram[0].rearrange("p c r -> p (c r)").bitcast(I32)
-
-        def load_weight(w, name, u):
-            rows = w.rearrange("(p j) c -> p j c", j=PACK)
-            raw = keep.tile([P, PACK, H // 2], F32, name="%s_raw%d" % (name, u), align_bytes=64)
-            nc.sync.dma_start(raw[:], rows[:, :, u * (H // 2) : (u + 1) * (H // 2)])
-            return raw
-
-        def round_weight(engines, halves, name):
+        def round_weight(parts, copies, name):
             grouped = keep.tile([P, PACK * H], BF16, name=name + "_bf", align_bytes=64)
             view = grouped[:].rearrange("p (t m j) -> p m j t", t=PACK, j=PACK)
-            for u in range(2):
-                dst = view[:, u * (P // 2) : (u + 1) * (P // 2), :, :]
-                src = halves[u][:].rearrange("p j (m t) -> p m j t", t=PACK)
-                if engines[u] == "scalar":
-                    nc.scalar.copy(dst, src)
-                elif engines[u] == "vector":
-                    nc.vector.tensor_copy(dst, src)
-                else:
-                    nc.gpsimd.tensor_scalar(dst, src, 1.0, 0.0, ALU.mult, ALU.add)
+            for copy, (raw, c0, c1) in zip(copies, parts):
+                copy(view[:, c0 // PACK : c1 // PACK, :, :], raw[:].rearrange("p j (m t) -> p m j t", t=PACK))
             return grouped
 
         def quantize(grouped, cuts, name):
@@ -76,24 +67,36 @@ def tile_picked_twqflowbstd_none_p_kernel(
                 nc.vector.quantize_mx(out=codes[:, a:b].bitcast(FP8X4), scales=scales[:, a:b], in_=grouped[:, PACK * a : PACK * b])
             return codes, scales
 
-        def pick(words, scales, lst, name, tag=None):
-            pw = keep.tile([P, S], U32, name=name + "_words", align_bytes=64)
-            ps = keep.tile([P, S], U8, name=name + "_bytes", tag=tag or name + "_bytes", align_bytes=64)
-            nc.vector.tensor_copy(pw[:], words[:].bitcast(U32).indirect(lst[:]))
-            nc.vector.tensor_copy(ps[:], scales[:].indirect(lst[:]))
-            return pw, ps
+        def pick(words, scales, lst, name, words_tag):
+            picked_words = keep.tile([P, S], U32, name=name + "_words", tag=words_tag, align_bytes=64)
+            picked_bytes = keep.tile([P, S], U8, name=name + "_bytes", align_bytes=64)
+            nc.vector.tensor_copy(picked_words[:], words[:].bitcast(U32).indirect(lst[:]))
+            nc.vector.tensor_copy(picked_bytes[:], scales[:].indirect(lst[:]))
+            return picked_words, picked_bytes
 
-        def product(dst, lhs, t, rhs, c0, n):
+        def product(dst, stationary, t, moving):
             cols = slice(t * P, (t + 1) * P)
             nc.tensor.matmul_mx(
                 out=dst,
-                lhsT=lhs[0][:, cols].bitcast(FP8X4),
-                lhsT_scale=lhs[1][:, cols],
-                rhs=rhs[0][:, c0 : c0 + n].bitcast(FP8X4),
-                rhs_scale=rhs[1][:, c0 : c0 + n],
+                lhsT=stationary[0][:, cols].bitcast(FP8X4),
+                lhsT_scale=stationary[1][:, cols],
+                rhs=moving[0][:].bitcast(FP8X4),
+                rhs_scale=moving[1][:],
                 start=True,
                 stop=True,
             )
+
+        def looked_up(window, lst, c0, n):
+            return window[:].indirect(lst[:, c0 // 16 : (c0 + n) // 16])
+
+        def leave_psum(on_vector, dst, src, scale):
+            if on_vector:
+                nc.vector.tensor_scalar(dst, src, scale, None, ALU.mult)
+            else:
+                nc.scalar.activation(dst, src, ACT.Copy, scale=scale)
+
+        def bank(i, name, n=S):
+            return psum.tile([P, n], F32, name=name, tag="bank%d" % i)
 
         l_offs = load_list(offs, "l_offs")
         l_two = load_list(two, "l_two")
@@ -102,19 +105,17 @@ def tile_picked_twqflowbstd_none_p_kernel(
         for a in range(4):
             queue = nc.sync if a == 0 else nc.scalar
             queue.dma_start(xs[a:P:4, :].bitcast(I32), x_rows[a].unsqueeze(1).to_broadcast([4, 8, T // 4]))
-        w1_raw = [load_weight(w1, "w1", 0)]
-        xw = keep.tile([P, T], I32, name="xw")
-        nc.sync.dma_start(xw[:], words_view(x_words))
-        w1_raw.append(load_weight(w1, "w1", 1))
-        w2_raw = [load_weight(w2, "w2", 0)]
+        w1_raw = [load_weight(w1, "w1_first", 0, W1_CUT)]
+        xw = load_words(x_words, T, "xw")
+        w1_raw.append(load_weight(w1, "w1_second", W1_CUT, H))
+        w2_raw = [load_weight(w2, "w2_first", 0, W2_CUT)]
         l_n1 = load_list(n1, "l_n1")
         l_n2 = load_list(n2, "l_n2")
-        w2_raw.append(load_weight(w2, "w2", 1))
+        w2_raw.append(load_weight(w2, "w2_second", W2_CUT, H))
         gain = keep.tile([P, PACK], F32, name="gain")
         nc.sync.dma_start(gain[:], gs.rearrange("(p t) o -> p (t o)", t=PACK))
         l_n3 = load_list(n3, "l_n3")
-        dw = keep.tile([P, G], I32, name="dw")
-        nc.sync.dma_start(dw[:], words_view(d_words))
+        dw = load_words(d_words, G, "dw")
         ds = keep.tile([P, G], U8, name="ds")
         nc.gpsimd.memset(ds[:].bitcast(I32), 0)
         for e in range(2):
@@ -123,195 +124,167 @@ def tile_picked_twqflowbstd_none_p_kernel(
         l_n4 = load_list(n4, "l_n4")
         l_n5 = load_list(n5, "l_n5")
 
+        warm = keep.tile([P, 2], F32, name="warm")
+        nc.gpsimd.memset(warm[:, 0:1], 1.0)
+        nc.scalar.activation(warm[:, 1:2], warm[:, 0:1], ACT.Abs_reciprocal_sqrt)
+
         ident = keep.tile([P, P], F32, name="ident")
         make_identity(nc, ident[:])
         dict_scales = keep.tile([P, H], U8, name="dict_scales", align_bytes=64)
         nc.gpsimd.memset(dict_scales[:].bitcast(I32), 0)
 
-        def bank(i, name):
-            return psum.tile([P, S], F32, name=name, tag="bank%d" % i)
-
-        def leave(engine, dst, src, scale):
-            if engine == "scalar":
-                nc.scalar.activation(dst, src, ACT.Copy, scale=scale)
-            else:
-                nc.vector.tensor_scalar(dst, src, scale, None, ALU.mult)
-
-        x_offs = pick(xw, xs, l_offs, "x_offs")
-        w1_q = quantize(round_weight(["scalar","scalar"], w1_raw, "w1"), [0, P, H], "w1")
+        x_offs = pick(xw, xs, l_offs, "x_offs", "x_offs_words")
+        w1_q = quantize(round_weight(w1_raw, [nc.scalar.copy, nc.scalar.copy], "w1"), [0, P, H], "w1")
         y_bank = [bank(t, "y_bank%d" % t) for t in range(PACK)]
         y_win = [keep.tile([P, S], F32, name="y_win%d" % t) for t in range(PACK)]
         for t in range(PACK):
-            product(y_bank[t][:], w1_q, t, x_offs, 0, S)
-            leave("vector" if t else "scalar", y_win[t][:], y_bank[t][:], 1.0)
+            product(y_bank[t][:], w1_q, t, x_offs)
+            leave_psum(t >= SCALAR_Y, y_win[t][:], y_bank[t][:], 1.0)
 
-        x_two = pick(xw, xs, l_two, "x_two")
-        w2_q = quantize(round_weight(["scalar","vector"], w2_raw, "w2"), [0, H], "w2")
-        half_gain = keep.tile([P, PACK], F32, name="half_gain")
-        nc.vector.tensor_scalar(half_gain[:], gain[:], 0.5, None, ALU.mult)
+        x_two = pick(xw, xs, l_two, "x_two", "w1_second")
+        w2_q = quantize(round_weight(w2_raw, [nc.scalar.copy, nc.vector.tensor_copy], "w2"), [0, H], "w2")
         d_bank = [bank(PACK + t, "d_bank%d" % t) for t in range(PACK)]
         d_win = [keep.tile([P, S], F32, name="d_win%d" % t) for t in range(PACK)]
         for t in range(PACK):
-            product(d_bank[t][:], w2_q, t, x_two, 0, S)
+            product(d_bank[t][:], w2_q, t, x_two)
 
-        def pick_dictionary():
-            dk_words, dk_bytes = pick(dw, ds, l_k1, "dk")
-            words = keep.tile([P, H], U32, name="dict_words", align_bytes=64)
-            nc.vector.tensor_copy(words[:].rearrange("p (t m) -> p m t", t=PACK), dk_words[:].rearrange("p (m t) -> p m t", t=PACK))
-            dealt = keep.tile([P, H], U8, name="dealt_bytes", align_bytes=64)
-            nc.vector.tensor_copy(dealt[:].rearrange("p (t m) -> p t m", t=PACK), dk_bytes[:].rearrange("p (m t) -> p t m", t=PACK))
-            for a in range(4):
-                nc.sync.dma_start(
-                    dict_scales[a:P:32, :].bitcast(I32), dealt[16 * (a // 2) + a % 2 : P : 32, :].bitcast(I32)
-                )
-            return words, dict_scales
+        dk_words, dk_bytes = pick(dw, ds, l_k1, "dk", "dk_words")
+        dict_words = keep.tile([P, H], U32, name="dict_words", align_bytes=64)
+        nc.vector.tensor_copy(dict_words[:].rearrange("p (t m) -> p t m", t=PACK), dk_words[:].rearrange("p (m t) -> p t m", t=PACK))
+        dealt_bytes = keep.tile([P, H], U8, name="dealt_bytes", align_bytes=64)
+        nc.vector.tensor_copy(dealt_bytes[:].rearrange("p (t m) -> p t m", t=PACK), dk_bytes[:].rearrange("p (m t) -> p t m", t=PACK))
+        for a in range(4):
+            nc.sync.dma_start(dict_scales[a:P:32, :].bitcast(I32), dealt_bytes[16 * (a // 2) + a % 2 : P : 32, :].bitcast(I32))
+        dictionary = (dict_words, dict_scales)
 
-        dictionary = None
-        z_q = []
-        sums = []
-        c0 = 0
-        for ci, n in enumerate(Z_CHUNKS):
-            last = ci == len(Z_CHUNKS) - 1
-            near = keep.tile([P, PACK, n], F32, name="near%d" % ci)
-            far = keep.tile([P, PACK, n], F32, name="far%d" % ci)
-            sums.append((near, far))
-            diffs, d3s = [], []
+        h_win = [keep.tile([P, 2 * S if t == WHOLE_TILE else S], F32, name="h_win%d" % t) for t in range(PACK)]
+        near = keep.tile([P, PACK, S], F32, name="near")
+        diffs = keep.tile([P, PACK, 2, S], F32, name="diffs")
 
-            def fetch_y(t):
-                y12 = ring.tile([P, 2, n], F32, name="y12", tag="y12", bufs=4)
-                gather("scalar", y12[:, 0, :], y_win[t], l_n1, c0, n)
-                gather("scalar", y12[:, 1, :], y_win[t], l_n2, c0, n)
-                if False:
-                    diff = sums[0][0][:, t, :].rearrange("p (s n) -> p s n", s=2)
-                else:
-                    diff_tile = keep.tile([P, 2, n], F32, name="diff%d%d" % (ci, t))
-                    diff = diff_tile[:]
-                if False:
-                    nc.gpsimd.tensor_tensor(diff, y12[:], y_win[t][:, c0 : c0 + n].unsqueeze(1).to_broadcast([P, 2, n]), ALU.subtract)
-                else:
-                    nc.vector.tensor_tensor(diff, y12[:], y_bank[t][:, c0 : c0 + n].unsqueeze(1).to_broadcast([P, 2, n]), ALU.subtract)
-                diffs.append(diff)
+        def fetched(name, shape):
+            return ring.tile(shape, F32, name=name, tag="fetched", bufs=PACK + 1)
 
-            def fetch_d(t):
-                d3 = ring.tile([P, n], F32, name="d3", tag="d3", bufs=4)
-                gather("scalar", d3[:], d_win[t], l_n3, c0, n)
-                d3s.append(d3)
-
-            def weigh(t):
+        def differences(u):
+            cols = slice(u * HALF, (u + 1) * HALF)
+            for t in range(PACK):
+                y12 = fetched("y12", [P, 2, HALF])
+                nc.scalar.activation(y12[:, 0, :], looked_up(y_win[t], l_n1, u * HALF, HALF), ACT.Copy)
+                nc.scalar.activation(y12[:, 1, :], looked_up(y_win[t], l_n2, u * HALF, HALF), ACT.Copy)
+                on_gpsimd = u == 0 and t < GPSIMD_DIFFS
+                y_here = y_win[t] if on_gpsimd else y_bank[t]
+                engine = nc.gpsimd if on_gpsimd else nc.vector
+                engine.tensor_tensor(diffs[:, t, :, cols], y12[:], y_here[:, cols].unsqueeze(1).to_broadcast([P, 2, HALF]), ALU.subtract)
                 nc.vector.scalar_tensor_tensor(
-                    near[:, t, :], d_bank[t][:, c0 : c0 + n], gain[:, t : t + 1], diffs[t][:, 0, :], ALU.mult, ALU.mult
+                    near[:, t, cols], d_bank[t][:, cols], gain[:, t : t + 1], diffs[:, t, 0, cols], ALU.mult, ALU.mult
                 )
-                far_engine = nc.vector
-                far_engine.tensor_tensor(far[:, t, :], d3s[t][:], diffs[t][:, 1, :], ALU.mult)
 
-            if ci == 0:
-                dictionary = pick_dictionary()
-                for t in range(PACK):
-                    fetch_y(t)
-                for t in range(PACK):
-                    leave("scalar", d_win[t][:], d_bank[t][:], half_gain[:, t : t + 1])
-                for t in range(PACK):
-                    fetch_d(t)
-                    weigh(t)
-            else:
-                for t in range(PACK):
-                    fetch_d(t)
-                    fetch_y(t)
-                    weigh(t)
-            z_bf = keep.tile([P, n * PACK], BF16, name="z_bf%d" % ci, align_bytes=64)
-            z_engine = nc.vector
-            z_engine.tensor_tensor(
+        def quantized_z(c0, n, d3, far, far_engine):
+            for t in range(PACK):
+                nc.scalar.activation(d3[:, t, :], looked_up(d_win[t], l_n3, c0, n), ACT.Copy, scale=0.5)
+                if t % 2:
+                    pair = slice(t - 1, t + 1)
+                    far_engine.tensor_tensor(far[:, pair, :], d3[:, pair, :], diffs[:, pair, 1, c0 : c0 + n], ALU.mult)
+            z_bf = keep.tile([P, n * PACK], BF16, name="z_bf%d" % c0, align_bytes=64)
+            nc.vector.tensor_tensor(
                 z_bf[:].rearrange("p (c i t) -> p c t i", i=4, t=PACK),
-                near[:].rearrange("p t (c i) -> p c t i", i=4),
-                far[:].rearrange("p t (c i) -> p c t i", i=4),
+                near[:, :, c0 : c0 + n].rearrange("p t (c i) -> p c t i", i=4),
+                far.rearrange("p t (c i) -> p c t i", i=4),
                 ALU.add,
             )
-            z_q.append((quantize(z_bf, [0, n], "z%d" % ci), c0, n))
-            c0 = c0 + n
+            return quantize(z_bf, [0, n], "z%d" % c0)
+
+        for t in range(PACK):
+            leave_psum(t >= SCALAR_D, d_win[t][:], d_bank[t][:], gain[:, t : t + 1])
+        differences(0)
+        d3_first = keep.tile([P, PACK, HALF], F32, name="d3_first")
+        far_first = keep.tile([P, PACK, HALF], F32, name="far_first")
+        z_first = quantized_z(0, HALF, d3_first, far_first[:], nc.gpsimd)
+        differences(1)
+        far_third = h_win[WHOLE_TILE][:, S:].rearrange("p (t n) -> p t n", t=PACK)
+        z_third = quantized_z(HALF, QUARTER, fetched("d3_third", [P, PACK, QUARTER]), far_third, nc.gpsimd)
+        far_last = keep.tile([P, PACK, QUARTER], F32, name="far_last")
+        z_last = quantized_z(HALF + QUARTER, QUARTER, fetched("d3_last", [P, PACK, QUARTER]), far_last[:], nc.vector)
 
         h_bank = [bank(t, "h_bank%d" % t) for t in range(PACK)]
-        h_win = [keep.tile([P, S], F32, name="h_win%d" % t) for t in range(PACK)]
-        early = S - Z_CHUNKS[-1]
         for t in range(PACK):
-            for zq, c0, n in z_q[:-1]:
-                product(h_bank[t][:, c0 : c0 + n], dictionary, t, zq, 0, n)
-            leave("scalar", h_win[t][:, :early], h_bank[t][:, :early], 0.0625)
+            product(h_bank[t][:, :HALF], dictionary, t, z_first)
+            leave_psum(False, h_win[t][:, :HALF], h_bank[t][:, :HALF], WIN_SCALE * H_SCALE)
         for t in range(PACK):
-            product(h_bank[t][:, early:], dictionary, t, z_q[-1][0], 0, S - early)
-            leave("vector" if t % 2 else "scalar", h_win[t][:, early:], h_bank[t][:, early:], 0.0625)
+            product(h_bank[t][:, HALF : HALF + QUARTER], dictionary, t, z_third)
+            product(h_bank[t][:, HALF + QUARTER :], dictionary, t, z_last)
+            leave_psum(t % 2 == 0, h_win[t][:, HALF:S], h_bank[t][:, HALF:], WIN_SCALE * H_SCALE)
 
         out_rows = out.rearrange("(p t) n -> p t n", t=PACK)
-        pieces = [(t, c0, HALF) for t in range(PACK) for c0 in (0, HALF)]
+        pieces = []
+        for t in range(PACK):
+            pieces.extend([(t, 0, S)] if t == WHOLE_TILE else [(t, 0, HALF), (t, HALF, HALF)])
         count = len(pieces)
-        used = {"both": {}, "apart": {}}
+        boths, terms, aparts = {}, {}, {}
+
+        def spent(tiles, j, n, name):
+            if j < count and pieces[j][2] >= n:
+                return tiles[j][:, :n]
+            fresh = ring.tile([P, n], F32, name=name)
+            return fresh[:]
 
         def fetch(i):
             t, c0, n = pieces[i]
             pa = ring.tile([P, n], F32, name="pa")
             pb = ring.tile([P, n], F32, name="pb")
-            gather("scalar", pa[:], h_win[t], l_n4, c0, n)
-            gather("scalar" if i in (1, 2) else "vector", pb[:], h_win[t], l_n5, c0, n)
+            nc.scalar.activation(pa[:], looked_up(h_win[t], l_n4, c0, n), ACT.Copy)
+            nc.vector.tensor_copy(pb[:], looked_up(h_win[t], l_n5, c0, n))
             return pa, pb
 
         def combine(i, pa, pb):
-            t, c0, n = pieces[i]
-            both = keep.tile([P, n], F32, name="both%d" % i)
-            apart = keep.tile([P, n], F32, name="apart%d" % i)
-            used["both"][i], used["apart"][i] = both, apart
-            both_engine = nc.vector if i in (0, count - 1) else nc.gpsimd
-            apart_engine = nc.vector if i in (0, count - 1) else nc.gpsimd
-            both_engine.tensor_tensor(both[:], pa[:], pb[:], ALU.add)
-            apart_engine.tensor_tensor(apart[:], pa[:], pb[:], ALU.subtract)
-            return both, apart
-
-        def square(i, both, apart):
-            t, c0, n = pieces[i]
-            h_here = h_bank[t][:, c0 : c0 + n]
-            top = ring.tile([P, n], F32, name="top", bufs=6)
-            mean = ring.tile([P, n], F32, name="mean")
-            nc.vector.scalar_tensor_tensor(mean[:], h_here, -5.0 / 48.0, both[:], ALU.mult, ALU.add)
-            nc.vector.scalar_tensor_tensor(top[:], h_here, -2.2 / 16.0, both[:], ALU.mult, ALU.add)
-            sq = ring.tile([P, 2, n], F32, name="sq")
-            nc.scalar.activation(sq[:, 0, :], apart[:], ACT.Square, scale=0.5**0.5)
-            nc.scalar.activation(sq[:, 1, :], mean[:], ACT.Square, scale=0.375 * 0.5**0.5)
-            if i >= count - 1:
-                total = ring.tile([P, n], F32, name="sum")
-                nc.vector.tensor_tensor(total[:], sq[:, 0, :], sq[:, 1, :], ALU.add)
-                return top, total[:]
-            total = psum.tile([P, n], F32, name="total", tag="bank%d" % (4 + i % 2))
-            for b in range(n // P):
-                for s in range(2):
-                    nc.tensor.matmul(
-                        total[:, b * P : (b + 1) * P], sq[:, s, b * P : (b + 1) * P], ident[:], start=(s == 0), stop=(s == 1), is_transpose=True
-                    )
-            return top, total[:]
-
-        def spent(kind, j, n, name):
-            if j < count and pieces[j][2] == n:
-                return used[kind][j]
-            return ring.tile([P, n], F32, name=name)
-
-        def invert(i, top, total):
-            t, c0, n = pieces[i]
-            root = spent("apart", i + 1, n, "root")
-            nc.scalar.activation(root[:], total, ACT.Abs_reciprocal_sqrt, bias=0.25)
-            if i >= count - 1:
-                return top, root[:]
-            back = psum.tile([P, n], F32, name="back", tag="bank%d" % (6 + i % 2))
-            for b in range(n // P):
-                nc.tensor.transpose(back[:, b * P : (b + 1) * P], root[:, b * P : (b + 1) * P], ident[:])
-            return top, back[:]
-
-        def finish(i, top, back):
-            t, c0, n = pieces[i]
-            res = spent("both", i + 3, n, "res")
-            nc.vector.scalar_tensor_tensor(res[:], top[:], -0.3125, back, ALU.mult, ALU.mult)
-            nc.sync.dma_start(out_rows[:, t, c0 : c0 + n], res[:])
+            n = pieces[i][2]
+            boths[i] = ring.tile([P, n], F32, name="both", bufs=5)
+            terms[i] = ring.tile([P, 2, n], F32, name="apart", bufs=4)
+            aparts[i] = terms[i][:, 0, :]
+            nc.gpsimd.tensor_tensor(boths[i][:], pa[:], pb[:], ALU.add)
+            nc.gpsimd.tensor_tensor(aparts[i], pa[:], pb[:], ALU.subtract)
             return ()
 
-        stages = [(square, 2), (invert, 3), (finish, 5), (combine, 1), (fetch, 0)]
+        def square(i):
+            t, c0, n = pieces[i]
+            sums = h_bank[t][:, c0 : c0 + n]
+            top = ring.tile([P, n], F32, name="top", bufs=4)
+            nc.vector.scalar_tensor_tensor(terms[i][:, 1, :], boths[i][:], -0.375, sums, ALU.mult, ALU.add)
+            nc.vector.scalar_tensor_tensor(top[:], boths[i][:], -0.625 / 2.2, sums, ALU.mult, ALU.add)
+            squares = ring.tile([P, 2, n], F32, name="squares")
+            nc.scalar.activation(squares[:], terms[i][:], ACT.Square)
+            if i == count - 1:
+                total = ring.tile([P, n], F32, name="total_plain")
+                nc.vector.tensor_tensor(total[:], squares[:, 0, :], squares[:, 1, :], ALU.add)
+                return top, total
+            total = bank(PACK + i % 2, "total_turned", n)
+            for b in range(n // P):
+                cols = slice(b * P, (b + 1) * P)
+                for s in range(2):
+                    nc.tensor.matmul(total[:, cols], squares[:, s, cols], ident[:], start=(s == 0), stop=(s == 1), is_transpose=True)
+            return top, total
+
+        def invert(i, top, total):
+            n = pieces[i][2]
+            root = spent(aparts, i + 1, n, "root")
+            nc.scalar.activation(root, total[:], ACT.Abs_reciprocal_sqrt, bias=0.25, scale=0.5 / WIN_SCALE**2)
+            if i == count - 1:
+                return top, root
+            back = bank(PACK + 2 + i % 2, "root_back", n)
+            for b in range(n // P):
+                cols = slice(b * P, (b + 1) * P)
+                nc.tensor.transpose(back[:, cols], root[:, cols], ident[:])
+            return top, back[:]
+
+        def finish(i, top, root):
+            t, c0, n = pieces[i]
+            result = spent(boths, i + 2, n, "result")
+            nc.vector.scalar_tensor_tensor(result, top[:], 0.6875 * H_SCALE, root, ALU.mult, ALU.mult)
+            nc.sync.dma_start(out_rows[:, t, c0 : c0 + n], result)
+            return ()
+
+        stages = [(square, 2), (invert, 3), (finish, 4), (combine, 1), (fetch, 0)]
         state = [()] * count
-        for step in range(count + 5):
+        for step in range(count + 4):
             for stage, lag in stages:
                 i = step - lag
                 if 0 <= i < count:

from contextlib import ExitStack

import concourse.mybir as mybir
from concourse.masks import make_identity

F32 = mybir.dt.float32
BF16 = mybir.dt.bfloat16
I32 = mybir.dt.int32
U32 = mybir.dt.uint32
U16 = mybir.dt.uint16
U8 = mybir.dt.uint8
FP8X4 = mybir.dt.float8_e4m3fn_x4
ACT = mybir.ActivationFunctionType
ALU = mybir.AluOpType

P = 128
PACK = 4
K, T, S, H, G = 512, 1024, 512, 512, 2048
HALF = S // 2
QUARTER = S // 4
H_SCALE = 0.0625
WIN_SCALE = 1.0 / (0.625 * H_SCALE)
FLOPS = 3 * 2 * K * H * S

WHOLE_TILE = 1
W1_CUT = 320
W2_CUT = H // 2
GPSIMD_DIFFS = 2
SCALAR_Y, SCALAR_D = 2, 1


def tile_picked_twqflowbstd_none_p_kernel(
    tc, x_words, x_scales, w1, w2, gs, d_words, d_scales, offs, two, n1, n2, n3, k1, n4, n5, out
):
    nc = tc.nc
    with ExitStack() as ctx:
        keep = ctx.enter_context(tc.tile_pool(name="keep", bufs=1))
        ring = ctx.enter_context(tc.tile_pool(name="ring", bufs=3))
        psum = ctx.enter_context(tc.psum_pool(name="psum", bufs=1))

        def load_list(src, name):
            tile = keep.tile([P, S // 16], U16, name=name)
            nc.sync.dma_start(tile[:], src)
            return tile

        def load_words(src, columns, name):
            tile = keep.tile([P, columns], I32, name=name)
            nc.sync.dma_start(tile[:], src[0].rearrange("p c r -> p (c r)").bitcast(I32))
            return tile

        def load_weight(w, name, c0, c1):
            raw = keep.tile([P, PACK, c1 - c0], F32, name=name, align_bytes=64)
            nc.sync.dma_start(raw[:], w.rearrange("(p j) c -> p j c", j=PACK)[:, :, c0:c1])
            return raw, c0, c1

        def round_weight(parts, copies, name):
            grouped = keep.tile([P, PACK * H], BF16, name=name + "_bf", align_bytes=64)
            view = grouped[:].rearrange("p (t m j) -> p m j t", t=PACK, j=PACK)
            for copy, (raw, c0, c1) in zip(copies, parts):
                copy(view[:, c0 // PACK : c1 // PACK, :, :], raw[:].rearrange("p j (m t) -> p m j t", t=PACK))
            return grouped

        def quantize(grouped, cuts, name):
            codes = keep.tile([P, cuts[-1]], U32, name=name + "_codes", align_bytes=64)
            scales = keep.tile([P, cuts[-1]], U8, name=name + "_scales", align_bytes=64)
            for a, b in zip(cuts, cuts[1:]):
                nc.vector.quantize_mx(out=codes[:, a:b].bitcast(FP8X4), scales=scales[:, a:b], in_=grouped[:, PACK * a : PACK * b])
            return codes, scales

        def pick(words, scales, lst, name, words_tag):
            picked_words = keep.tile([P, S], U32, name=name + "_words", tag=words_tag, align_bytes=64)
            picked_bytes = keep.tile([P, S], U8, name=name + "_bytes", align_bytes=64)
            nc.vector.tensor_copy(picked_words[:], words[:].bitcast(U32).indirect(lst[:]))
            nc.vector.tensor_copy(picked_bytes[:], scales[:].indirect(lst[:]))
            return picked_words, picked_bytes

        def product(dst, stationary, t, moving):
            cols = slice(t * P, (t + 1) * P)
            nc.tensor.matmul_mx(
                out=dst,
                lhsT=stationary[0][:, cols].bitcast(FP8X4),
                lhsT_scale=stationary[1][:, cols],
                rhs=moving[0][:].bitcast(FP8X4),
                rhs_scale=moving[1][:],
                start=True,
                stop=True,
            )

        def looked_up(window, lst, c0, n):
            return window[:].indirect(lst[:, c0 // 16 : (c0 + n) // 16])

        def leave_psum(on_vector, dst, src, scale):
            if on_vector:
                nc.vector.tensor_scalar(dst, src, scale, None, ALU.mult)
            else:
                nc.scalar.activation(dst, src, ACT.Copy, scale=scale)

        def bank(i, name, n=S):
            return psum.tile([P, n], F32, name=name, tag="bank%d" % i)

        l_offs = load_list(offs, "l_offs")
        l_two = load_list(two, "l_two")
        xs = keep.tile([P, T], U8, name="xs")
        x_rows = x_scales[0].bitcast(I32).rearrange("(q a) c -> a q c", a=4)
        for a in range(4):
            queue = nc.sync if a == 0 else nc.scalar
            queue.dma_start(xs[a:P:4, :].bitcast(I32), x_rows[a].unsqueeze(1).to_broadcast([4, 8, T // 4]))
        w1_raw = [load_weight(w1, "w1_first", 0, W1_CUT)]
        xw = load_words(x_words, T, "xw")
        w1_raw.append(load_weight(w1, "w1_second", W1_CUT, H))
        w2_raw = [load_weight(w2, "w2_first", 0, W2_CUT)]
        l_n1 = load_list(n1, "l_n1")
        l_n2 = load_list(n2, "l_n2")
        w2_raw.append(load_weight(w2, "w2_second", W2_CUT, H))
        gain = keep.tile([P, PACK], F32, name="gain")
        nc.sync.dma_start(gain[:], gs.rearrange("(p t) o -> p (t o)", t=PACK))
        l_n3 = load_list(n3, "l_n3")
        dw = load_words(d_words, G, "dw")
        ds = keep.tile([P, G], U8, name="ds")
        nc.gpsimd.memset(ds[:].bitcast(I32), 0)
        for e in range(2):
            nc.sync.dma_start(ds[e:P:16, :].bitcast(I32), d_scales[0, e:16:2, :].bitcast(I32))
        l_k1 = load_list(k1, "l_k1")
        l_n4 = load_list(n4, "l_n4")
        l_n5 = load_list(n5, "l_n5")

        warm = keep.tile([P, 2], F32, name="warm")
        nc.gpsimd.memset(warm[:, 0:1], 1.0)
        nc.scalar.activation(warm[:, 1:2], warm[:, 0:1], ACT.Abs_reciprocal_sqrt)

        ident = keep.tile([P, P], F32, name="ident")
        make_identity(nc, ident[:])
        dict_scales = keep.tile([P, H], U8, name="dict_scales", align_bytes=64)
        nc.gpsimd.memset(dict_scales[:].bitcast(I32), 0)

        x_offs = pick(xw, xs, l_offs, "x_offs", "x_offs_words")
        w1_q = quantize(round_weight(w1_raw, [nc.scalar.copy, nc.scalar.copy], "w1"), [0, P, H], "w1")
        y_bank = [bank(t, "y_bank%d" % t) for t in range(PACK)]
        y_win = [keep.tile([P, S], F32, name="y_win%d" % t) for t in range(PACK)]
        for t in range(PACK):
            product(y_bank[t][:], w1_q, t, x_offs)
            leave_psum(t >= SCALAR_Y, y_win[t][:], y_bank[t][:], 1.0)

        x_two = pick(xw, xs, l_two, "x_two", "w1_second")
        w2_q = quantize(round_weight(w2_raw, [nc.scalar.copy, nc.vector.tensor_copy], "w2"), [0, H], "w2")
        d_bank = [bank(PACK + t, "d_bank%d" % t) for t in range(PACK)]
        d_win = [keep.tile([P, S], F32, name="d_win%d" % t) for t in range(PACK)]
        for t in range(PACK):
            product(d_bank[t][:], w2_q, t, x_two)

        dk_words, dk_bytes = pick(dw, ds, l_k1, "dk", "dk_words")
        dict_words = keep.tile([P, H], U32, name="dict_words", align_bytes=64)
        nc.vector.tensor_copy(dict_words[:].rearrange("p (t m) -> p t m", t=PACK), dk_words[:].rearrange("p (m t) -> p t m", t=PACK))
        dealt_bytes = keep.tile([P, H], U8, name="dealt_bytes", align_bytes=64)
        nc.vector.tensor_copy(dealt_bytes[:].rearrange("p (t m) -> p t m", t=PACK), dk_bytes[:].rearrange("p (m t) -> p t m", t=PACK))
        for a in range(4):
            nc.sync.dma_start(dict_scales[a:P:32, :].bitcast(I32), dealt_bytes[16 * (a // 2) + a % 2 : P : 32, :].bitcast(I32))
        dictionary = (dict_words, dict_scales)

        h_win = [keep.tile([P, 2 * S if t == WHOLE_TILE else S], F32, name="h_win%d" % t) for t in range(PACK)]
        near = keep.tile([P, PACK, S], F32, name="near")
        diffs = keep.tile([P, PACK, 2, S], F32, name="diffs")

        def fetched(name, shape):
            return ring.tile(shape, F32, name=name, tag="fetched", bufs=PACK + 1)

        def differences(u):
            cols = slice(u * HALF, (u + 1) * HALF)
            for t in range(PACK):
                y12 = fetched("y12", [P, 2, HALF])
                nc.scalar.activation(y12[:, 0, :], looked_up(y_win[t], l_n1, u * HALF, HALF), ACT.Copy)
                nc.scalar.activation(y12[:, 1, :], looked_up(y_win[t], l_n2, u * HALF, HALF), ACT.Copy)
                on_gpsimd = u == 0 and t < GPSIMD_DIFFS
                y_here = y_win[t] if on_gpsimd else y_bank[t]
                engine = nc.gpsimd if on_gpsimd else nc.vector
                engine.tensor_tensor(diffs[:, t, :, cols], y12[:], y_here[:, cols].unsqueeze(1).to_broadcast([P, 2, HALF]), ALU.subtract)
                nc.vector.scalar_tensor_tensor(
                    near[:, t, cols], d_bank[t][:, cols], gain[:, t : t + 1], diffs[:, t, 0, cols], ALU.mult, ALU.mult
                )

        def quantized_z(c0, n, d3, far, far_engine):
            for t in range(PACK):
                nc.scalar.activation(d3[:, t, :], looked_up(d_win[t], l_n3, c0, n), ACT.Copy, scale=0.5)
                if t % 2:
                    pair = slice(t - 1, t + 1)
                    far_engine.tensor_tensor(far[:, pair, :], d3[:, pair, :], diffs[:, pair, 1, c0 : c0 + n], ALU.mult)
            z_bf = keep.tile([P, n * PACK], BF16, name="z_bf%d" % c0, align_bytes=64)
            nc.vector.tensor_tensor(
                z_bf[:].rearrange("p (c i t) -> p c t i", i=4, t=PACK),
                near[:, :, c0 : c0 + n].rearrange("p t (c i) -> p c t i", i=4),
                far.rearrange("p t (c i) -> p c t i", i=4),
                ALU.add,
            )
            return quantize(z_bf, [0, n], "z%d" % c0)

        for t in range(PACK):
            leave_psum(t >= SCALAR_D, d_win[t][:], d_bank[t][:], gain[:, t : t + 1])
        differences(0)
        d3_first = keep.tile([P, PACK, HALF], F32, name="d3_first")
        far_first = keep.tile([P, PACK, HALF], F32, name="far_first")
        z_first = quantized_z(0, HALF, d3_first, far_first[:], nc.gpsimd)
        differences(1)
        far_third = h_win[WHOLE_TILE][:, S:].rearrange("p (t n) -> p t n", t=PACK)
        z_third = quantized_z(HALF, QUARTER, fetched("d3_third", [P, PACK, QUARTER]), far_third, nc.gpsimd)
        far_last = keep.tile([P, PACK, QUARTER], F32, name="far_last")
        z_last = quantized_z(HALF + QUARTER, QUARTER, fetched("d3_last", [P, PACK, QUARTER]), far_last[:], nc.vector)

        h_bank = [bank(t, "h_bank%d" % t) for t in range(PACK)]
        for t in range(PACK):
            product(h_bank[t][:, :HALF], dictionary, t, z_first)
            leave_psum(False, h_win[t][:, :HALF], h_bank[t][:, :HALF], WIN_SCALE * H_SCALE)
        for t in range(PACK):
            product(h_bank[t][:, HALF : HALF + QUARTER], dictionary, t, z_third)
            product(h_bank[t][:, HALF + QUARTER :], dictionary, t, z_last)
            leave_psum(t % 2 == 0, h_win[t][:, HALF:S], h_bank[t][:, HALF:], WIN_SCALE * H_SCALE)

        out_rows = out.rearrange("(p t) n -> p t n", t=PACK)
        pieces = []
        for t in range(PACK):
            pieces.extend([(t, 0, S)] if t == WHOLE_TILE else [(t, 0, HALF), (t, HALF, HALF)])
        count = len(pieces)
        boths, terms, aparts = {}, {}, {}

        def spent(tiles, j, n, name):
            if j < count and pieces[j][2] >= n:
                return tiles[j][:, :n]
            fresh = ring.tile([P, n], F32, name=name)
            return fresh[:]

        def fetch(i):
            t, c0, n = pieces[i]
            pa = ring.tile([P, n], F32, name="pa")
            pb = ring.tile([P, n], F32, name="pb")
            nc.scalar.activation(pa[:], looked_up(h_win[t], l_n4, c0, n), ACT.Copy)
            nc.vector.tensor_copy(pb[:], looked_up(h_win[t], l_n5, c0, n))
            return pa, pb

        def combine(i, pa, pb):
            n = pieces[i][2]
            boths[i] = ring.tile([P, n], F32, name="both", bufs=5)
            terms[i] = ring.tile([P, 2, n], F32, name="apart", bufs=4)
            aparts[i] = terms[i][:, 0, :]
            nc.gpsimd.tensor_tensor(boths[i][:], pa[:], pb[:], ALU.add)
            nc.gpsimd.tensor_tensor(aparts[i], pa[:], pb[:], ALU.subtract)
            return ()

        def square(i):
            t, c0, n = pieces[i]
            sums = h_bank[t][:, c0 : c0 + n]
            top = ring.tile([P, n], F32, name="top", bufs=4)
            nc.vector.scalar_tensor_tensor(terms[i][:, 1, :], boths[i][:], -0.375, sums, ALU.mult, ALU.add)
            nc.vector.scalar_tensor_tensor(top[:], boths[i][:], -0.625 / 2.2, sums, ALU.mult, ALU.add)
            squares = ring.tile([P, 2, n], F32, name="squares")
            nc.scalar.activation(squares[:], terms[i][:], ACT.Square)
            if i == count - 1:
                total = ring.tile([P, n], F32, name="total_plain")
                nc.vector.tensor_tensor(total[:], squares[:, 0, :], squares[:, 1, :], ALU.add)
                return top, total
            total = bank(PACK + i % 2, "total_turned", n)
            for b in range(n // P):
                cols = slice(b * P, (b + 1) * P)
                for s in range(2):
                    nc.tensor.matmul(total[:, cols], squares[:, s, cols], ident[:], start=(s == 0), stop=(s == 1), is_transpose=True)
            return top, total

        def invert(i, top, total):
            n = pieces[i][2]
            root = spent(aparts, i + 1, n, "root")
            nc.scalar.activation(root, total[:], ACT.Abs_reciprocal_sqrt, bias=0.25, scale=0.5 / WIN_SCALE**2)
            if i == count - 1:
                return top, root
            back = bank(PACK + 2 + i % 2, "root_back", n)
            for b in range(n // P):
                cols = slice(b * P, (b + 1) * P)
                nc.tensor.transpose(back[:, cols], root[:, cols], ident[:])
            return top, back[:]

        def finish(i, top, root):
            t, c0, n = pieces[i]
            result = spent(boths, i + 2, n, "result")
            nc.vector.scalar_tensor_tensor(result, top[:], 0.6875 * H_SCALE, root, ALU.mult, ALU.mult)
            nc.sync.dma_start(out_rows[:, t, c0 : c0 + n], result)
            return ()

        stages = [(square, 2), (invert, 3), (finish, 4), (combine, 1), (fetch, 0)]
        state = [()] * count
        for step in range(count + 4):
            for stage, lag in stages:
                i = step - lag
                if 0 <= i < count:
                    state[i] = stage(i, *state[i])
